import numpy as np
import ml_dtypes


def mxq(x, axis, fmt="e4m3"):
    dtype, down = {"e4m3": (ml_dtypes.float8_e4m3fn, 7), "e5m2": (ml_dtypes.float8_e5m2, 14)}[fmt]
    v = np.moveaxis(np.asarray(x, np.float32).astype(ml_dtypes.bfloat16).astype(np.float64), axis, -1)
    blocks = v.reshape(v.shape[:-1] + (-1, 32))
    amax = np.abs(blocks).max(-1, keepdims=True)
    byte = np.maximum(np.where(amax > 0, np.frexp(amax)[1] - 1 + 127, 0) - down, 1)
    scale = np.exp2(byte - 127.0)
    codes = (blocks / scale).astype(np.float32).astype(dtype).astype(np.float64)
    return np.moveaxis((codes * scale).reshape(v.shape), -1, axis)


WIDE = False


def mx_kscale(k):
    if not WIDE:
        return np.ones(k)
    levels = np.array([10, -10, 5, -5, 0])
    if k % 512:
        return np.exp2(np.random.permutation(np.resize(levels, k // 32))).repeat(32)
    a = np.empty((k // 512, 16))
    for p in range(k // 512):
        a[p, :8] = np.random.permutation(np.resize(levels, 8))
        for g in range(8):
            far = levels[np.abs(levels - a[p, g]) >= 10]
            a[p, g + 8] = far[np.random.randint(len(far))]
    return np.exp2(a.ravel()).repeat(32)


def f64(x):
    return np.asarray(x).astype(np.float64)


def striped(idx):
    return np.tile(idx.reshape(-1, 16).T, (8, 1)).astype(np.uint16)


def unstriped(offs):
    return offs[:16].T.reshape(-1).astype(np.int64)


def pack_weight(w):
    k, n = w.shape
    w = f64(np.asarray(w, np.float32).astype(ml_dtypes.bfloat16)).reshape(k // 32, 32, n)
    amax = np.abs(w).max(1)
    byte = np.clip(np.where(amax > 0, np.frexp(amax)[1] - 1 + 127 - 7, 1), 1, 254)
    scaled = (w * np.exp2(127.0 - byte)[:, None, :]).reshape(k, n).astype(np.float32)
    words = np.ascontiguousarray(scaled.reshape(k // 512, 128, 4, n).transpose(0, 1, 3, 2)).astype(ml_dtypes.float8_e4m3fn).view(np.uint8)
    return words, np.ascontiguousarray(byte.astype(np.uint8).reshape(k // 512, 16, n))


def unpack_weight(words, scales):
    g, p, n, _ = words.shape
    vals = np.ascontiguousarray(words).view(ml_dtypes.float8_e4m3fn).astype(np.float64) * np.repeat(np.exp2(scales.astype(np.float64) - 127.0), 8, axis=1)[..., None]
    return vals.transpose(0, 1, 3, 2).reshape(g * 512, n)


def relu(v):
    return np.maximum(v, 0.0)


K, T, S, H, N, D, U, W = 512, 2048, 512, 512, 256, 8, 512, 1024
P = 2 ** 7


def setup_inputs():
    n = np.random.standard_normal
    s = mx_kscale(K)[:, None]
    u = mx_kscale(H)
    packed_xT = pack_weight(n((K, T)) * s)
    packed_eT = pack_weight(n((K, W)) * s)
    return {
        "x_words": packed_xT[0],
        "x_scales": packed_xT[1],
        "e_words": packed_eT[0],
        "e_scales": packed_eT[1],
        "w1": (n((K, H)) / np.sqrt(K) / s * u).astype(np.float32),
        "w2": (n((K, H)) / np.sqrt(K) / s).astype(np.float32),
        "w3": (n((H, N)) / np.sqrt(H) / u[:, None]).astype(np.float32),
        "bias": (0.5 * n((H, 1)) + 0.3).astype(np.float32),
        "risk": (np.tile(np.random.uniform(0.2, 1.0, U), (P, 1))).astype(np.float32),
        "offs": striped(np.random.permutation(T)[:S]),
        "tau": striped(np.random.permutation(W)[:U]),
        "whose": striped(np.random.randint(0, S, U)),
    }


def reference(x_words, x_scales, e_words, e_scales, w1, w2, w3, bias, risk, offs, tau, whose):
    xq = unpack_weight(x_words, x_scales)[:, unstriped(offs)]
    h = relu(mxq(f64(w1), 0, "e4m3").T @ xq)
    e_tau = unpack_weight(e_words, e_scales)[:, unstriped(tau)]
    phi = relu((mxq(f64(w2), 0, "e4m3").T @ e_tau) + f64(bias))
    z = h[:, unstriped(whose)] * phi
    qv = mxq(f64(w3), 0, "e4m3").T @ mxq(z, 0, "e4m3")
    qw = qv * f64(risk)[:1]
    return (qw.reshape(len(qw), -1, D).sum(axis=2)) / (f64(risk)[:1].reshape(len(f64(risk)[:1]), -1, D).sum(axis=2))

@@ -1,0 +1,223 @@
+from contextlib import ExitStack
+
+import concourse.mybir as mybir
+from concourse.masks import make_identity
+
+K, T, W, S, H, N, D, U = 512, 2048, 1024, 512, 512, 256, 8, 512
+FLOPS = 2 * K * H * S + 2 * K * H * U + 2 * H * N * U
+
+F32 = mybir.dt.float32
+BF16 = mybir.dt.bfloat16
+I32 = mybir.dt.int32
+U32 = mybir.dt.uint32
+U16 = mybir.dt.uint16
+U8 = mybir.dt.uint8
+FP8X4 = mybir.dt.float8_e4m3fn_x4
+ACT = mybir.ActivationFunctionType
+ALU = mybir.AluOpType
+AXIS = mybir.AxisListType
+
+P = 128
+PACK = 4
+HALVES = 2
+HALF = U // HALVES
+TILES = HALF // P
+
+
+def tile_picked_yiqn_risk_p_kernel(
+    tc, x_words, x_scales, e_words, e_scales, w1, w2, w3, bias, risk, offs, tau, whose, out
+):
+    nc = tc.nc
+    with ExitStack() as ctx:
+        keep = ctx.enter_context(tc.tile_pool(name="keep", bufs=1))
+        late = ctx.enter_context(tc.tile_pool(name="late", bufs=1))
+        psum = ctx.enter_context(tc.psum_pool(name="psum", bufs=1))
+
+        def sb(shape, dtype, name):
+            return keep.tile(shape, dtype, name=name, align_bytes=64)
+
+        def bank(index, shape):
+            return psum.tile(shape, F32, name="bank%d" % index)
+
+        offs_sb = keep.tile([P, S // 16], U16, name="offs_sb")
+        tau_sb = keep.tile([P, U // 16], U16, name="tau_sb")
+        whose_sb = keep.tile([P, U // 16], U16, name="whose_sb")
+        x_plane = sb([P, T], U8, "x_plane")
+        e_plane = sb([P, W], U8, "e_plane")
+        w1_raw = sb([P, PACK, H], F32, "w1_raw")
+        identity = sb([P, P], F32, "identity")
+
+        scratch = late.tile([P, 4160], F32, name="scratch", align_bytes=64, offset=0)
+        x_table = sb([P, T], U32, "x_table")
+        e_table = late.tile([P, W], U32, name="e_table", align_bytes=64, offset=0)
+        w2_raw = late.tile([P, PACK, H], F32, name="w2_raw", align_bytes=64, offset=4 * W)
+        w3_raw = late.tile([P, PACK, N], F32, name="w3_raw", align_bytes=64, offset=4 * (W + PACK * H))
+        small = 4 * (W + PACK * H + PACK * N)
+        bias_sb = late.tile([P, PACK], F32, name="bias_sb", align_bytes=64, offset=small)
+        risk_own = late.tile([P, HALVES, TILES], F32, name="risk_own", align_bytes=64, offset=small + 64)
+        risk_group = late.tile([P, HALVES, D], F32, name="risk_group", align_bytes=64, offset=small + 128)
+        nc.gpsimd.memset(x_plane[:].bitcast(U32), 0)
+        nc.vector.memset(e_plane[:].bitcast(U32), 0)
+        make_identity(nc, scratch[:, :P])
+        nc.vector.tensor_copy(out=identity[:], in_=scratch[:, :P])
+
+        def load_plane(queue, plane, scales):
+            for q in range(4):
+                queue.dma_start(out=plane[32 * q : 32 * q + 4, :].bitcast(I32), in_=scales[0, 4 * q : 4 * q + 4, :].bitcast(I32))
+
+        def load_words(table, words):
+            nc.sync.dma_start(out=table[:].bitcast(I32), in_=words[0].rearrange("p n t -> p (n t)").bitcast(I32))
+
+        def load_weight(raw, w):
+            nc.sync.dma_start(out=raw[:], in_=w.rearrange("(p j) c -> p j c", j=PACK))
+
+        nc.sync.dma_start(offs_sb[:], offs)
+        load_weight(w1_raw, w1)
+        nc.sync.dma_start(tau_sb[:], tau)
+        load_plane(nc.scalar, x_plane, x_scales)
+        load_words(x_table, x_words)
+        nc.sync.dma_start(whose_sb[:], whose)
+        load_plane(nc.gpsimd, e_plane, e_scales)
+        load_words(e_table, e_words)
+        load_weight(w2_raw, w2)
+        load_weight(w3_raw, w3)
+        nc.sync.dma_start(out=bias_sb[:], in_=bias.rearrange("(p t) o -> p (t o)", t=PACK))
+        nc.sync.dma_start(out=risk_own[:], in_=risk[0].rearrange("(c p j) -> p c j", c=HALVES, j=TILES))
+        share = D // TILES
+        for q in range(share):
+            nc.sync.dma_start(out=risk_group[q:P:share], in_=risk[1 + q].rearrange("(c v d) -> v c d", c=HALVES, d=D))
+
+        def cast_dealt(raw, name, vector_cols):
+            staged = sb([P, PACK, P, PACK], BF16, name)
+            src = raw[:].rearrange("p j (m t) -> p m j t", t=PACK)
+            dst = staged[:].rearrange("p t m j -> p m j t")
+            if vector_cols:
+                nc.vector.tensor_copy(out=dst[:, :vector_cols], in_=src[:, :vector_cols])
+            nc.scalar.copy(out=dst[:, vector_cols:], in_=src[:, vector_cols:])
+            return staged
+
+        def quantize(staged_flat, width, name):
+            codes = sb([P, width], U32, name + "_codes")
+            scales = sb([P, width], U8, name + "_scales")
+            nc.vector.quantize_mx(out=codes[:].bitcast(FP8X4), scales=scales[:], in_=staged_flat)
+            return codes, scales
+
+        def pick(table, plane, offsets, codes_slot, scales_slot):
+            codes = sb([P, S], U32, codes_slot)
+            scales = sb([P, S], U8, scales_slot)
+            nc.vector.tensor_copy(out=scales[:], in_=plane[:].indirect(offsets[:]))
+            nc.vector.tensor_copy(out=codes[:], in_=table[:].indirect(offsets[:]))
+            return codes, scales
+
+        def product(acc, stationary, cols, moving):
+            nc.tensor.matmul_mx(
+                out=acc,
+                lhsT=stationary[0][:, cols].bitcast(FP8X4),
+                lhsT_scale=stationary[1][:, cols],
+                rhs=moving[0][:].bitcast(FP8X4),
+                rhs_scale=moving[1][:],
+                start=True,
+                stop=True,
+            )
+
+        w1_staged = cast_dealt(w1_raw, "w1_staged", 84)
+        w1_q = quantize(w1_staged[:].rearrange("p t m j -> p (t m j)"), H, "w1")
+        x_q = pick(x_table, x_plane, offs_sb, "x_codes", "w1_staged")
+        h = []
+        for t in range(PACK):
+            acc = bank(t, [P, S])
+            product(acc[:], w1_q, slice(t * P, (t + 1) * P), x_q)
+            h_t = sb([P, S], F32, "h%d" % t)
+            nc.scalar.activation(out=h_t[:], in_=acc[:], func=ACT.Relu)
+            h.append(h_t)
+
+        e_q = pick(e_table, e_plane, tau_sb, "e_codes", "x_table")
+        w2_staged = cast_dealt(w2_raw, "w2_staged", 0)
+        w2_q = quantize(w2_staged[:].rearrange("p t m j -> p (t m j)"), H, "w2")
+        pre = []
+        for t in range(PACK):
+            acc = bank(PACK + t, [P, U])
+            product(acc[:], w2_q, slice(t * P, (t + 1) * P), e_q)
+            pre.append(acc)
+
+        fetched = {}
+        for c in range(HALVES):
+            for t in range(PACK):
+                if (c, t) == (1, 2):
+                    last = sb([P, 2, HALF], F32, "w2_staged")
+                g = last[:, t - 2, :] if c == 1 and t >= 2 else sb([P, HALF], F32, "fetched%d_%d" % (c, t))[:]
+                cols = slice(c * HALF // 16, (c + 1) * HALF // 16)
+                nc.vector.tensor_copy(out=g, in_=h[t][:].indirect(whose_sb[:, cols]))
+                fetched[c, t] = g
+
+        w3_staged = late.tile([P, N, PACK], BF16, name="w3_staged", align_bytes=64, offset=4 * W)
+        nc.scalar.copy(
+            out=w3_staged[:].rearrange("p (n i) j -> p n j i", i=4),
+            in_=w3_raw[:].rearrange("p j (n i) -> p n j i", i=4),
+        )
+        w3_q = quantize(w3_staged[:].rearrange("p n j -> p (n j)"), N, "w3")
+
+        total = sb([P, HALVES], F32, "h0")
+        nc.vector.tensor_reduce(out=total[:], in_=risk_group[:], axis=AXIS.X, op=ALU.add)
+        inverse = sb([P, HALVES], F32, "inverse")
+        nc.vector.reciprocal(out=inverse[:], in_=total[:])
+        weight = sb([P, HALVES, TILES], F32, "weight")
+        nc.vector.tensor_tensor(
+            out=weight[:], in0=risk_own[:], in1=inverse[:].unsqueeze(2).to_broadcast([P, HALVES, TILES]), op=ALU.mult
+        )
+
+        result = sb([P, N // P, U // D], F32, "result")
+        groups = HALF // D
+        for c in range(HALVES):
+            planar = sb([P, PACK, HALF], BF16, "planar%d" % c)
+            for t in range(PACK):
+                nc.vector.scalar_tensor_tensor(
+                    out=planar[:, t, :],
+                    in0=pre[t][:, c * HALF : (c + 1) * HALF],
+                    scalar=bias_sb[:, t : t + 1],
+                    in1=fetched[c, t],
+                    op0=ALU.add,
+                    op1=ALU.mult,
+                )
+            z = sb([P, TILES, P, PACK], BF16, "z%d" % c)
+            src = planar[:].rearrange("p t (m j) -> p m t j", j=TILES)
+            dst = z[:].rearrange("p j m t -> p m t j")
+            if c == 0:
+                nc.scalar.activation(out=dst, in_=src, func=ACT.Relu)
+            else:
+                nc.vector.tensor_scalar(out=dst[:, :88], in0=src[:, :88], scalar1=0.0, scalar2=None, op0=ALU.max)
+                nc.scalar.activation(out=dst[:, 88:], in_=src[:, 88:], func=ACT.Relu)
+            z_q = quantize(z[:].rearrange("p j m t -> p (j m t)"), HALF, "z%d" % c)
+            weighted = []
+            if c == 0:
+                both = bank(0, [P, TILES, N])
+            accs = []
+            for j in range(TILES):
+                acc = both[:, j, :] if c == 0 else bank(2 + j, [P, N])[:]
+                product(acc, z_q, slice(j * P, (j + 1) * P), w3_q)
+                accs.append(acc)
+            for j, acc in enumerate(accs):
+                scaled = sb([P, N], F32, "scaled%d_%d" % (c, j))
+                if c == 1 and j == 1:
+                    nc.vector.tensor_scalar(out=scaled[:], in0=acc, scalar1=weight[:, c, j : j + 1], scalar2=None, op0=ALU.mult)
+                else:
+                    nc.scalar.activation(out=scaled[:], in_=acc, func=ACT.Copy, scale=weight[:, c, j : j + 1])
+                weighted.append(scaled)
+            turned = bank(1 if c == 0 else PACK, [P, N // P, P])
+            for mh in range(N // P):
+                for j in range(TILES):
+                    nc.tensor.matmul(
+                        turned[:, mh, :],
+                        lhsT=weighted[j][:, mh * P : (mh + 1) * P],
+                        rhs=identity[:],
+                        is_transpose=True,
+                        start=(j == 0),
+                        stop=(j == TILES - 1),
+                    )
+            nc.vector.tensor_reduce(
+                out=result[:, :, c * groups : (c + 1) * groups],
+                in_=turned[:].rearrange("p h (v s) -> p h v s", s=share),
+                axis=AXIS.X,
+                op=ALU.add,
+            )
+        nc.sync.dma_start(out=out.rearrange("(h p) v -> p h v", p=P), in_=result[:])

@@ -22,6 +22,7 @@ PACK = 4
 HALVES = 2
 HALF = U // HALVES
 TILES = HALF // P
+WINDOW = 688
 
 
 def tile_picked_yiqn_risk_p_kernel(
@@ -43,23 +44,26 @@ def tile_picked_yiqn_risk_p_kernel(
         tau_sb = keep.tile([P, U // 16], U16, name="tau_sb")
         whose_sb = keep.tile([P, U // 16], U16, name="whose_sb")
         x_plane = sb([P, T], U8, "x_plane")
-        e_plane = sb([P, W], U8, "e_plane")
         w1_raw = sb([P, PACK, H], F32, "w1_raw")
         identity = sb([P, P], F32, "identity")
 
-        scratch = late.tile([P, 4160], F32, name="scratch", align_bytes=64, offset=0)
-        x_table = sb([P, T], U32, "x_table")
-        e_table = late.tile([P, W], U32, name="e_table", align_bytes=64, offset=0)
-        w2_raw = late.tile([P, PACK, H], F32, name="w2_raw", align_bytes=64, offset=4 * W)
-        w3_raw = late.tile([P, PACK, N], F32, name="w3_raw", align_bytes=64, offset=4 * (W + PACK * H))
-        small = 4 * (W + PACK * H + PACK * N)
-        bias_sb = late.tile([P, PACK], F32, name="bias_sb", align_bytes=64, offset=small)
-        risk_own = late.tile([P, HALVES, TILES], F32, name="risk_own", align_bytes=64, offset=small + 64)
-        risk_group = late.tile([P, HALVES, D], F32, name="risk_group", align_bytes=64, offset=small + 128)
-        nc.gpsimd.memset(x_plane[:].bitcast(U32), 0)
+        late_bytes = [4 * T, W, 4 * W, 4 * PACK * H, 4 * PACK * N]
+        starts = [sum(late_bytes[:i]) for i in range(len(late_bytes))]
+        scratch = late.tile([P, sum(late_bytes) // 4], F32, name="scratch", align_bytes=64, offset=0)
+        x_table = late.tile([P, T], U32, name="x_table", align_bytes=64, offset=starts[0])
+        e_plane = late.tile([P, W], U8, name="e_plane", align_bytes=64, offset=starts[1])
+        e_table = late.tile([P, W], U32, name="e_table", align_bytes=64, offset=starts[2])
+        w2_raw = late.tile([P, PACK, H], F32, name="w2_raw", align_bytes=64, offset=starts[3])
+        w3_raw = late.tile([P, PACK, N], F32, name="w3_raw", align_bytes=64, offset=starts[4])
+        bias_sb = sb([P, PACK], F32, "bias_sb")
+        risk_group = sb([P, 2, D], F32, "risk_group")
+        make_identity(nc, identity[:])
+        h = [sb([P, WINDOW], F32, "h%d" % t) for t in range(PACK)]
+        nc.vector.memset(scratch[:, : WINDOW - S], 0.0)
+        nc.vector.memset(x_plane[:].bitcast(U32), 0)
+        for t in range(PACK):
+            nc.vector.tensor_copy(out=h[t][:, S:], in_=scratch[:, : WINDOW - S])
         nc.vector.memset(e_plane[:].bitcast(U32), 0)
-        make_identity(nc, scratch[:, :P])
-        nc.vector.tensor_copy(out=identity[:], in_=scratch[:, :P])
 
         def load_plane(queue, plane, scales):
             for q in range(4):
@@ -72,29 +76,25 @@ def tile_picked_yiqn_risk_p_kernel(
             nc.sync.dma_start(out=raw[:], in_=w.rearrange("(p j) c -> p j c", j=PACK))
 
         nc.sync.dma_start(offs_sb[:], offs)
-        load_weight(w1_raw, w1)
         nc.sync.dma_start(tau_sb[:], tau)
+        nc.sync.dma_start(whose_sb[:], whose)
+        load_weight(w1_raw, w1)
         load_plane(nc.scalar, x_plane, x_scales)
         load_words(x_table, x_words)
-        nc.sync.dma_start(whose_sb[:], whose)
-        load_plane(nc.gpsimd, e_plane, e_scales)
+        load_plane(nc.sync, e_plane, e_scales)
         load_words(e_table, e_words)
         load_weight(w2_raw, w2)
         load_weight(w3_raw, w3)
-        nc.sync.dma_start(out=bias_sb[:], in_=bias.rearrange("(p t) o -> p (t o)", t=PACK))
-        nc.sync.dma_start(out=risk_own[:], in_=risk[0].rearrange("(c p j) -> p c j", c=HALVES, j=TILES))
-        share = D // TILES
-        for q in range(share):
-            nc.sync.dma_start(out=risk_group[q:P:share], in_=risk[1 + q].rearrange("(c v d) -> v c d", c=HALVES, d=D))
+        nc.gpsimd.dma_start(out=bias_sb[:], in_=bias.rearrange("(p t) o -> p (t o)", t=PACK))
+        for q in range(2):
+            for other in range(2):
+                row = risk[2 * q + other].rearrange("(v c e j) -> v e c j", c=HALVES, e=2, j=TILES)
+                nc.gpsimd.dma_start(out=risk_group[q:P:2, other, : D // 2].rearrange("p (c j) -> p c j", j=TILES), in_=row[:, (q + other) % 2])
 
-        def cast_dealt(raw, name, vector_cols):
-            staged = sb([P, PACK, P, PACK], BF16, name)
+        def dealt(raw, staged, first):
             src = raw[:].rearrange("p j (m t) -> p m j t", t=PACK)
-            dst = staged[:].rearrange("p t m j -> p m j t")
-            if vector_cols:
-                nc.vector.tensor_copy(out=dst[:, :vector_cols], in_=src[:, :vector_cols])
-            nc.scalar.copy(out=dst[:, vector_cols:], in_=src[:, vector_cols:])
-            return staged
+            dst = staged[:].rearrange("p t m j -> p m j t")[:, first : first + src.shape[1]]
+            return dst, src
 
         def quantize(staged_flat, width, name):
             codes = sb([P, width], U32, name + "_codes")
@@ -120,19 +120,21 @@ def tile_picked_yiqn_risk_p_kernel(
                 stop=True,
             )
 
-        w1_staged = cast_dealt(w1_raw, "w1_staged", 84)
+        w1_staged = sb([P, PACK, P, PACK], BF16, "w1_staged")
+        dst, src = dealt(w1_raw, w1_staged, 0)
+        nc.vector.tensor_copy(out=dst[:, :40], in_=src[:, :40])
+        nc.scalar.copy(out=dst[:, 40:], in_=src[:, 40:])
         w1_q = quantize(w1_staged[:].rearrange("p t m j -> p (t m j)"), H, "w1")
-        x_q = pick(x_table, x_plane, offs_sb, "x_codes", "w1_staged")
-        h = []
+        x_q = pick(x_table, x_plane, offs_sb, "x_codes", "x_picked_scales")
         for t in range(PACK):
             acc = bank(t, [P, S])
             product(acc[:], w1_q, slice(t * P, (t + 1) * P), x_q)
-            h_t = sb([P, S], F32, "h%d" % t)
-            nc.scalar.activation(out=h_t[:], in_=acc[:], func=ACT.Relu)
-            h.append(h_t)
+            nc.scalar.activation(out=h[t][:, :S], in_=acc[:], func=ACT.Relu)
 
-        e_q = pick(e_table, e_plane, tau_sb, "e_codes", "x_table")
-        w2_staged = cast_dealt(w2_raw, "w2_staged", 0)
+        e_q = pick(e_table, e_plane, tau_sb, "e_codes", "e_picked_scales")
+        w2_staged = sb([P, PACK, P, PACK], BF16, "x_codes")
+        dst, src = dealt(w2_raw, w2_staged, 0)
+        nc.scalar.copy(out=dst, in_=src)
         w2_q = quantize(w2_staged[:].rearrange("p t m j -> p (t m j)"), H, "w2")
         pre = []
         for t in range(PACK):
@@ -140,42 +142,39 @@ def tile_picked_yiqn_risk_p_kernel(
             product(acc[:], w2_q, slice(t * P, (t + 1) * P), e_q)
             pre.append(acc)
 
-        fetched = {}
-        for c in range(HALVES):
-            for t in range(PACK):
-                if (c, t) == (1, 2):
-                    last = sb([P, 2, HALF], F32, "w2_staged")
-                g = last[:, t - 2, :] if c == 1 and t >= 2 else sb([P, HALF], F32, "fetched%d_%d" % (c, t))[:]
-                cols = slice(c * HALF // 16, (c + 1) * HALF // 16)
-                nc.vector.tensor_copy(out=g, in_=h[t][:].indirect(whose_sb[:, cols]))
-                fetched[c, t] = g
+        fetched = []
+        for t in range(PACK):
+            if t == 0:
+                g = late.tile([P, U], F32, name="fetched0", align_bytes=64, offset=starts[2])
+            else:
+                g = sb([P, U], F32, "x_codes" if t == PACK - 1 else "fetched%d" % t)
+            nc.vector.tensor_copy(out=g[:], in_=h[t][:].indirect(whose_sb[:]))
+            fetched.append(g)
 
-        w3_staged = late.tile([P, N, PACK], BF16, name="w3_staged", align_bytes=64, offset=4 * W)
+        w3_staged = late.tile([P, N, PACK], BF16, name="w3_staged", align_bytes=64, offset=starts[3])
         nc.scalar.copy(
             out=w3_staged[:].rearrange("p (n i) j -> p n j i", i=4),
             in_=w3_raw[:].rearrange("p j (n i) -> p n j i", i=4),
         )
         w3_q = quantize(w3_staged[:].rearrange("p n j -> p (n j)"), N, "w3")
 
-        total = sb([P, HALVES], F32, "h0")
-        nc.vector.tensor_reduce(out=total[:], in_=risk_group[:], axis=AXIS.X, op=ALU.add)
-        inverse = sb([P, HALVES], F32, "inverse")
+        total = sb([P, 1], F32, "e_codes")
+        nc.vector.tensor_reduce(out=total[:], in_=risk_group[:, :, : D // 2], axis=AXIS.XY, op=ALU.add)
+        inverse = sb([P, 1], F32, "inverse")
         nc.vector.reciprocal(out=inverse[:], in_=total[:])
-        weight = sb([P, HALVES, TILES], F32, "weight")
-        nc.vector.tensor_tensor(
-            out=weight[:], in0=risk_own[:], in1=inverse[:].unsqueeze(2).to_broadcast([P, HALVES, TILES]), op=ALU.mult
-        )
+        weight = sb([P, HALVES * TILES], F32, "weight")
+        nc.vector.tensor_scalar(out=weight[:], in0=risk_group[:, 0, : D // 2], scalar1=inverse[:], scalar2=None, op0=ALU.mult)
 
         result = sb([P, N // P, U // D], F32, "result")
-        groups = HALF // D
+        turned = [bank(1 + 2 * mh, [P, P]) for mh in range(N // P)]
         for c in range(HALVES):
             planar = sb([P, PACK, HALF], BF16, "planar%d" % c)
             for t in range(PACK):
                 nc.vector.scalar_tensor_tensor(
-                    out=planar[:, t, :],
-                    in0=pre[t][:, c * HALF : (c + 1) * HALF],
+                    out=planar[:, t, :].rearrange("p (v d) -> p v d", d=D // HALVES),
+                    in0=pre[t][:].rearrange("p (v c d) -> p c v d", c=HALVES, d=D // HALVES)[:, c],
                     scalar=bias_sb[:, t : t + 1],
-                    in1=fetched[c, t],
+                    in1=fetched[t][:].rearrange("p (v c d) -> p c v d", c=HALVES, d=D // HALVES)[:, c],
                     op0=ALU.add,
                     op1=ALU.mult,
                 )
@@ -189,34 +188,32 @@ def tile_picked_yiqn_risk_p_kernel(
                 nc.scalar.activation(out=dst[:, 88:], in_=src[:, 88:], func=ACT.Relu)
             z_q = quantize(z[:].rearrange("p j m t -> p (j m t)"), HALF, "z%d" % c)
             weighted = []
-            if c == 0:
-                both = bank(0, [P, TILES, N])
             accs = []
             for j in range(TILES):
-                acc = both[:, j, :] if c == 0 else bank(2 + j, [P, N])[:]
+                acc = bank(2 * j if c == 0 else PACK + j, [P, N])[:]
                 product(acc, z_q, slice(j * P, (j + 1) * P), w3_q)
                 accs.append(acc)
             for j, acc in enumerate(accs):
                 scaled = sb([P, N], F32, "scaled%d_%d" % (c, j))
                 if c == 1 and j == 1:
-                    nc.vector.tensor_scalar(out=scaled[:], in0=acc, scalar1=weight[:, c, j : j + 1], scalar2=None, op0=ALU.mult)
+                    nc.vector.tensor_scalar(out=scaled[:], in0=acc, scalar1=weight[:, TILES * c + j : TILES * c + j + 1], scalar2=None, op0=ALU.mult)
                 else:
-                    nc.scalar.activation(out=scaled[:], in_=acc, func=ACT.Copy, scale=weight[:, c, j : j + 1])
+                    nc.scalar.activation(out=scaled[:], in_=acc, func=ACT.Copy, scale=weight[:, TILES * c + j : TILES * c + j + 1])
                 weighted.append(scaled)
-            turned = bank(1 if c == 0 else PACK, [P, N // P, P])
             for mh in range(N // P):
                 for j in range(TILES):
                     nc.tensor.matmul(
-                        turned[:, mh, :],
+                        turned[mh][:],
                         lhsT=weighted[j][:, mh * P : (mh + 1) * P],
                         rhs=identity[:],
                         is_transpose=True,
-                        start=(j == 0),
-                        stop=(j == TILES - 1),
+                        start=(c == 0 and j == 0),
+                        stop=(c == HALVES - 1 and j == TILES - 1),
                     )
+        for mh in range(N // P):
             nc.vector.tensor_reduce(
-                out=result[:, :, c * groups : (c + 1) * groups],
-                in_=turned[:].rearrange("p h (v s) -> p h v s", s=share),
+                out=result[:, mh, :],
+                in_=turned[mh][:].rearrange("p (v s) -> p v s", s=2),
                 axis=AXIS.X,
                 op=ALU.add,
             )

@@ -45,19 +45,18 @@ def tile_picked_yiqn_risk_p_kernel(
         whose_sb = keep.tile([P, U // 16], U16, name="whose_sb")
         x_plane = sb([P, T], U8, "x_plane")
         w1_raw = sb([P, PACK, H], F32, "w1_raw")
-        identity = sb([P, P], F32, "identity")
 
-        late_bytes = [4 * T, W, 4 * W, 4 * PACK * H, 4 * PACK * N]
+        late_bytes = [4 * T, 4 * P, 4 * W, 4 * PACK * H, 4 * PACK * N, 64, 64, W]
         starts = [sum(late_bytes[:i]) for i in range(len(late_bytes))]
         scratch = late.tile([P, sum(late_bytes) // 4], F32, name="scratch", align_bytes=64, offset=0)
         x_table = late.tile([P, T], U32, name="x_table", align_bytes=64, offset=starts[0])
-        e_plane = late.tile([P, W], U8, name="e_plane", align_bytes=64, offset=starts[1])
+        identity = late.tile([P, P], F32, name="identity", align_bytes=64, offset=starts[1])
         e_table = late.tile([P, W], U32, name="e_table", align_bytes=64, offset=starts[2])
         w2_raw = late.tile([P, PACK, H], F32, name="w2_raw", align_bytes=64, offset=starts[3])
         w3_raw = late.tile([P, PACK, N], F32, name="w3_raw", align_bytes=64, offset=starts[4])
-        bias_sb = sb([P, PACK], F32, "bias_sb")
-        risk_group = sb([P, 2, D], F32, "risk_group")
-        make_identity(nc, identity[:])
+        bias_sb = late.tile([P, PACK], F32, name="bias_sb", align_bytes=64, offset=starts[5])
+        risk_group = late.tile([P, 2, D], F32, name="risk_group", align_bytes=64, offset=starts[6])
+        e_plane = late.tile([P, W], U8, name="e_plane", align_bytes=64, offset=starts[7])
         h = [sb([P, WINDOW], F32, "h%d" % t) for t in range(PACK)]
         nc.vector.memset(scratch[:, : WINDOW - S], 0.0)
         nc.vector.memset(x_plane[:].bitcast(U32), 0)
@@ -65,8 +64,8 @@ def tile_picked_yiqn_risk_p_kernel(
             nc.vector.tensor_copy(out=h[t][:, S:], in_=scratch[:, : WINDOW - S])
         nc.vector.memset(e_plane[:].bitcast(U32), 0)
 
-        def load_plane(queue, plane, scales):
-            for q in range(4):
+        def load_plane(queues, plane, scales):
+            for q, queue in enumerate(queues):
                 queue.dma_start(out=plane[32 * q : 32 * q + 4, :].bitcast(I32), in_=scales[0, 4 * q : 4 * q + 4, :].bitcast(I32))
 
         def load_words(table, words):
@@ -79,9 +78,9 @@ def tile_picked_yiqn_risk_p_kernel(
         nc.sync.dma_start(tau_sb[:], tau)
         nc.sync.dma_start(whose_sb[:], whose)
         load_weight(w1_raw, w1)
-        load_plane(nc.scalar, x_plane, x_scales)
+        load_plane([nc.scalar] * 4, x_plane, x_scales)
         load_words(x_table, x_words)
-        load_plane(nc.sync, e_plane, e_scales)
+        load_plane([nc.sync] * 4, e_plane, e_scales)
         load_words(e_table, e_words)
         load_weight(w2_raw, w2)
         load_weight(w3_raw, w3)
@@ -90,6 +89,8 @@ def tile_picked_yiqn_risk_p_kernel(
             for other in range(2):
                 row = risk[2 * q + other].rearrange("(v c e j) -> v e c j", c=HALVES, e=2, j=TILES)
                 nc.gpsimd.dma_start(out=risk_group[q:P:2, other, : D // 2].rearrange("p (c j) -> p c j", j=TILES), in_=row[:, (q + other) % 2])
+
+        make_identity(nc, identity[:])
 
         def dealt(raw, staged, first):
             src = raw[:].rearrange("p j (m t) -> p m j t", t=PACK)
@@ -134,7 +135,8 @@ def tile_picked_yiqn_risk_p_kernel(
         e_q = pick(e_table, e_plane, tau_sb, "e_codes", "e_picked_scales")
         w2_staged = sb([P, PACK, P, PACK], BF16, "x_codes")
         dst, src = dealt(w2_raw, w2_staged, 0)
-        nc.scalar.copy(out=dst, in_=src)
+        nc.vector.tensor_copy(out=dst[:, :16], in_=src[:, :16])
+        nc.scalar.copy(out=dst[:, 16:], in_=src[:, 16:])
         w2_q = quantize(w2_staged[:].rearrange("p t m j -> p (t m j)"), H, "w2")
         pre = []
         for t in range(PACK):
@@ -151,19 +153,12 @@ def tile_picked_yiqn_risk_p_kernel(
             nc.vector.tensor_copy(out=g[:], in_=h[t][:].indirect(whose_sb[:]))
             fetched.append(g)
 
-        w3_staged = late.tile([P, N, PACK], BF16, name="w3_staged", align_bytes=64, offset=starts[3])
-        nc.scalar.copy(
-            out=w3_staged[:].rearrange("p (n i) j -> p n j i", i=4),
-            in_=w3_raw[:].rearrange("p j (n i) -> p n j i", i=4),
-        )
-        w3_q = quantize(w3_staged[:].rearrange("p n j -> p (n j)"), N, "w3")
-
-        total = sb([P, 1], F32, "e_codes")
-        nc.vector.tensor_reduce(out=total[:], in_=risk_group[:, :, : D // 2], axis=AXIS.XY, op=ALU.add)
-        inverse = sb([P, 1], F32, "inverse")
-        nc.vector.reciprocal(out=inverse[:], in_=total[:])
-        weight = sb([P, HALVES * TILES], F32, "weight")
-        nc.vector.tensor_scalar(out=weight[:], in0=risk_group[:, 0, : D // 2], scalar1=inverse[:], scalar2=None, op0=ALU.mult)
+        quad = sb([P, 4], F32, "quad")
+        nc.gpsimd.tensor_tensor(out=quad[:], in0=risk_group[:, 0, :4], in1=risk_group[:, 1, :4], op=ALU.add)
+        pair = sb([P, 2], F32, "pair")
+        nc.gpsimd.tensor_tensor(out=pair[:], in0=quad[:, :2], in1=quad[:, 2:], op=ALU.add)
+        total = sb([P, 1], F32, "total")
+        nc.gpsimd.tensor_tensor(out=total[:], in0=pair[:, :1], in1=pair[:, 1:], op=ALU.add)
 
         result = sb([P, N // P, U // D], F32, "result")
         turned = [bank(1 + 2 * mh, [P, P]) for mh in range(N // P)]
@@ -178,6 +173,19 @@ def tile_picked_yiqn_risk_p_kernel(
                     op0=ALU.add,
                     op1=ALU.mult,
                 )
+            if c == 0:
+                inverse = sb([P, 1], F32, "w2_scales")
+                nc.vector.reciprocal(out=inverse[:], in_=total[:])
+                weight = sb([P, HALVES * TILES], F32, "weight")
+                nc.gpsimd.tensor_scalar(
+                    out=weight[:], in0=risk_group[:, 0, :4], scalar1=inverse[:], scalar2=0.0, op0=ALU.mult, op1=ALU.add
+                )
+                w3_staged = sb([P, N, PACK], BF16, "e_codes")
+                nc.scalar.copy(
+                    out=w3_staged[:].rearrange("p (n i) j -> p n j i", i=4),
+                    in_=w3_raw[:].rearrange("p j (n i) -> p n j i", i=4),
+                )
+                w3_q = quantize(w3_staged[:].rearrange("p n j -> p (n j)"), N, "w3")
             z = sb([P, TILES, P, PACK], BF16, "z%d" % c)
             src = planar[:].rearrange("p t (m j) -> p m t j", j=TILES)
             dst = z[:].rearrange("p j m t -> p m t j")
@@ -195,13 +203,13 @@ def tile_picked_yiqn_risk_p_kernel(
                 accs.append(acc)
             for j, acc in enumerate(accs):
                 scaled = sb([P, N], F32, "scaled%d_%d" % (c, j))
-                if c == 1 and j == 1:
+                if j == 1:
                     nc.vector.tensor_scalar(out=scaled[:], in0=acc, scalar1=weight[:, TILES * c + j : TILES * c + j + 1], scalar2=None, op0=ALU.mult)
                 else:
                     nc.scalar.activation(out=scaled[:], in_=acc, func=ACT.Copy, scale=weight[:, TILES * c + j : TILES * c + j + 1])
                 weighted.append(scaled)
-            for mh in range(N // P):
-                for j in range(TILES):
+            for j in range(TILES):
+                for mh in range(N // P):
                     nc.tensor.matmul(
                         turned[mh][:],
                         lhsT=weighted[j][:, mh * P : (mh + 1) * P],

@@ -135,8 +135,7 @@ def tile_picked_yiqn_risk_p_kernel(
         e_q = pick(e_table, e_plane, tau_sb, "e_codes", "e_picked_scales")
         w2_staged = sb([P, PACK, P, PACK], BF16, "x_codes")
         dst, src = dealt(w2_raw, w2_staged, 0)
-        nc.vector.tensor_copy(out=dst[:, :16], in_=src[:, :16])
-        nc.scalar.copy(out=dst[:, 16:], in_=src[:, 16:])
+        nc.scalar.copy(out=dst, in_=src)
         w2_q = quantize(w2_staged[:].rearrange("p t m j -> p (t m j)"), H, "w2")
         pre = []
         for t in range(PACK):
@@ -152,6 +151,13 @@ def tile_picked_yiqn_risk_p_kernel(
                 g = sb([P, U], F32, "x_codes" if t == PACK - 1 else "fetched%d" % t)
             nc.vector.tensor_copy(out=g[:], in_=h[t][:].indirect(whose_sb[:]))
             fetched.append(g)
+
+        w3_staged = late.tile([P, N // P, P, PACK], BF16, name="w3_staged", align_bytes=64, offset=starts[3])
+        nc.scalar.copy(
+            out=w3_staged[:].rearrange("p h m j -> p m j h"),
+            in_=w3_raw[:].rearrange("p j (m h) -> p m j h", h=N // P),
+        )
+        w3_q = quantize(w3_staged[:].rearrange("p h m j -> p (h m j)"), N, "w3")
 
         quad = sb([P, 4], F32, "quad")
         nc.gpsimd.tensor_tensor(out=quad[:], in0=risk_group[:, 0, :4], in1=risk_group[:, 1, :4], op=ALU.add)
@@ -180,12 +186,6 @@ def tile_picked_yiqn_risk_p_kernel(
                 nc.gpsimd.tensor_scalar(
                     out=weight[:], in0=risk_group[:, 0, :4], scalar1=inverse[:], scalar2=0.0, op0=ALU.mult, op1=ALU.add
                 )
-                w3_staged = sb([P, N, PACK], BF16, "e_codes")
-                nc.scalar.copy(
-                    out=w3_staged[:].rearrange("p (n i) j -> p n j i", i=4),
-                    in_=w3_raw[:].rearrange("p j (n i) -> p n j i", i=4),
-                )
-                w3_q = quantize(w3_staged[:].rearrange("p n j -> p (n j)"), N, "w3")
             z = sb([P, TILES, P, PACK], BF16, "z%d" % c)
             src = planar[:].rearrange("p t (m j) -> p m t j", j=TILES)
             dst = z[:].rearrange("p j m t -> p m t j")
@@ -225,4 +225,4 @@ def tile_picked_yiqn_risk_p_kernel(
                 axis=AXIS.X,
                 op=ALU.add,
             )
-        nc.sync.dma_start(out=out.rearrange("(h p) v -> p h v", p=P), in_=result[:])
+        nc.sync.dma_start(out=out.rearrange("(p h) v -> p h v", p=P), in_=result[:])

@@ -84,11 +84,11 @@ def tile_picked_yiqn_risk_p_kernel(
         load_words(e_table, e_words)
         load_weight(w2_raw, w2)
         load_weight(w3_raw, w3)
-        nc.gpsimd.dma_start(out=bias_sb[:], in_=bias.rearrange("(p t) o -> p (t o)", t=PACK))
+        nc.sync.dma_start(out=bias_sb[:], in_=bias.rearrange("(p t) o -> p (t o)", t=PACK))
         for q in range(2):
             for other in range(2):
                 row = risk[2 * q + other].rearrange("(v c e j) -> v e c j", c=HALVES, e=2, j=TILES)
-                nc.gpsimd.dma_start(out=risk_group[q:P:2, other, : D // 2].rearrange("p (c j) -> p c j", j=TILES), in_=row[:, (q + other) % 2])
+                nc.sync.dma_start(out=risk_group[q:P:2, other, : D // 2].rearrange("p (c j) -> p c j", j=TILES), in_=row[:, (q + other) % 2])
 
         make_identity(nc, identity[:])
 
@@ -180,7 +180,7 @@ def tile_picked_yiqn_risk_p_kernel(
                     op1=ALU.mult,
                 )
             if c == 0:
-                inverse = sb([P, 1], F32, "w2_scales")
+                inverse = late.tile([P, 1], F32, name="inverse", align_bytes=64, offset=starts[3])
                 nc.vector.reciprocal(out=inverse[:], in_=total[:])
                 weight = sb([P, HALVES * TILES], F32, "weight")
                 nc.gpsimd.tensor_scalar(

from contextlib import ExitStack

import concourse.mybir as mybir
from concourse.masks import make_identity

K, T, W, S, H, N, D, U = 512, 2048, 1024, 512, 512, 256, 8, 512
FLOPS = 2 * K * H * S + 2 * K * H * U + 2 * H * N * U

F32 = mybir.dt.float32
BF16 = mybir.dt.bfloat16
I32 = mybir.dt.int32
U32 = mybir.dt.uint32
U16 = mybir.dt.uint16
U8 = mybir.dt.uint8
FP8X4 = mybir.dt.float8_e4m3fn_x4
ACT = mybir.ActivationFunctionType
ALU = mybir.AluOpType
AXIS = mybir.AxisListType

P = 128
PACK = 4
HALVES = 2
HALF = U // HALVES
TILES = HALF // P
WINDOW = 688


def tile_picked_yiqn_risk_p_kernel(
    tc, x_words, x_scales, e_words, e_scales, w1, w2, w3, bias, risk, offs, tau, whose, out
):
    nc = tc.nc
    with ExitStack() as ctx:
        keep = ctx.enter_context(tc.tile_pool(name="keep", bufs=1))
        late = ctx.enter_context(tc.tile_pool(name="late", bufs=1))
        psum = ctx.enter_context(tc.psum_pool(name="psum", bufs=1))

        def sb(shape, dtype, name):
            return keep.tile(shape, dtype, name=name, align_bytes=64)

        def bank(index, shape):
            return psum.tile(shape, F32, name="bank%d" % index)

        offs_sb = keep.tile([P, S // 16], U16, name="offs_sb")
        tau_sb = keep.tile([P, U // 16], U16, name="tau_sb")
        whose_sb = keep.tile([P, U // 16], U16, name="whose_sb")
        x_plane = sb([P, T], U8, "x_plane")
        w1_raw = sb([P, PACK, H], F32, "w1_raw")

        late_bytes = [4 * T, 4 * P, 4 * W, 4 * PACK * H, 4 * PACK * N, 64, 64, W]
        starts = [sum(late_bytes[:i]) for i in range(len(late_bytes))]
        scratch = late.tile([P, sum(late_bytes) // 4], F32, name="scratch", align_bytes=64, offset=0)
        x_table = late.tile([P, T], U32, name="x_table", align_bytes=64, offset=starts[0])
        identity = late.tile([P, P], F32, name="identity", align_bytes=64, offset=starts[1])
        e_table = late.tile([P, W], U32, name="e_table", align_bytes=64, offset=starts[2])
        w2_raw = late.tile([P, PACK, H], F32, name="w2_raw", align_bytes=64, offset=starts[3])
        w3_raw = late.tile([P, PACK, N], F32, name="w3_raw", align_bytes=64, offset=starts[4])
        bias_sb = late.tile([P, PACK], F32, name="bias_sb", align_bytes=64, offset=starts[5])
        risk_group = late.tile([P, 2, D], F32, name="risk_group", align_bytes=64, offset=starts[6])
        e_plane = late.tile([P, W], U8, name="e_plane", align_bytes=64, offset=starts[7])
        h = [sb([P, WINDOW], F32, "h%d" % t) for t in range(PACK)]
        nc.vector.memset(scratch[:, : WINDOW - S], 0.0)
        nc.vector.memset(x_plane[:].bitcast(U32), 0)
        for t in range(PACK):
            nc.vector.tensor_copy(out=h[t][:, S:], in_=scratch[:, : WINDOW - S])
        nc.vector.memset(e_plane[:].bitcast(U32), 0)

        def load_plane(queues, plane, scales):
            for q, queue in enumerate(queues):
                queue.dma_start(out=plane[32 * q : 32 * q + 4, :].bitcast(I32), in_=scales[0, 4 * q : 4 * q + 4, :].bitcast(I32))

        def load_words(table, words):
            nc.sync.dma_start(out=table[:].bitcast(I32), in_=words[0].rearrange("p n t -> p (n t)").bitcast(I32))

        def load_weight(raw, w):
            nc.sync.dma_start(out=raw[:], in_=w.rearrange("(p j) c -> p j c", j=PACK))

        nc.sync.dma_start(offs_sb[:], offs)
        nc.sync.dma_start(tau_sb[:], tau)
        nc.sync.dma_start(whose_sb[:], whose)
        load_weight(w1_raw, w1)
        load_plane([nc.scalar] * 4, x_plane, x_scales)
        load_words(x_table, x_words)
        load_plane([nc.sync] * 4, e_plane, e_scales)
        load_words(e_table, e_words)
        load_weight(w2_raw, w2)
        load_weight(w3_raw, w3)
        nc.sync.dma_start(out=bias_sb[:], in_=bias.rearrange("(p t) o -> p (t o)", t=PACK))
        for q in range(2):
            for other in range(2):
                row = risk[2 * q + other].rearrange("(v c e j) -> v e c j", c=HALVES, e=2, j=TILES)
                nc.sync.dma_start(out=risk_group[q:P:2, other, : D // 2].rearrange("p (c j) -> p c j", j=TILES), in_=row[:, (q + other) % 2])

        make_identity(nc, identity[:])

        def dealt(raw, staged, first):
            src = raw[:].rearrange("p j (m t) -> p m j t", t=PACK)
            dst = staged[:].rearrange("p t m j -> p m j t")[:, first : first + src.shape[1]]
            return dst, src

        def quantize(staged_flat, width, name):
            codes = sb([P, width], U32, name + "_codes")
            scales = sb([P, width], U8, name + "_scales")
            nc.vector.quantize_mx(out=codes[:].bitcast(FP8X4), scales=scales[:], in_=staged_flat)
            return codes, scales

        def pick(table, plane, offsets, codes_slot, scales_slot):
            codes = sb([P, S], U32, codes_slot)
            scales = sb([P, S], U8, scales_slot)
            nc.vector.tensor_copy(out=scales[:], in_=plane[:].indirect(offsets[:]))
            nc.vector.tensor_copy(out=codes[:], in_=table[:].indirect(offsets[:]))
            return codes, scales

        def product(acc, stationary, cols, moving):
            nc.tensor.matmul_mx(
                out=acc,
                lhsT=stationary[0][:, cols].bitcast(FP8X4),
                lhsT_scale=stationary[1][:, cols],
                rhs=moving[0][:].bitcast(FP8X4),
                rhs_scale=moving[1][:],
                start=True,
                stop=True,
            )

        w1_staged = sb([P, PACK, P, PACK], BF16, "w1_staged")
        dst, src = dealt(w1_raw, w1_staged, 0)
        nc.vector.tensor_copy(out=dst[:, :40], in_=src[:, :40])
        nc.scalar.copy(out=dst[:, 40:], in_=src[:, 40:])
        w1_q = quantize(w1_staged[:].rearrange("p t m j -> p (t m j)"), H, "w1")
        x_q = pick(x_table, x_plane, offs_sb, "x_codes", "x_picked_scales")
        for t in range(PACK):
            acc = bank(t, [P, S])
            product(acc[:], w1_q, slice(t * P, (t + 1) * P), x_q)
            nc.scalar.activation(out=h[t][:, :S], in_=acc[:], func=ACT.Relu)

        e_q = pick(e_table, e_plane, tau_sb, "e_codes", "e_picked_scales")
        w2_staged = sb([P, PACK, P, PACK], BF16, "x_codes")
        dst, src = dealt(w2_raw, w2_staged, 0)
        nc.scalar.copy(out=dst, in_=src)
        w2_q = quantize(w2_staged[:].rearrange("p t m j -> p (t m j)"), H, "w2")
        pre = []
        for t in range(PACK):
            acc = bank(PACK + t, [P, U])
            product(acc[:], w2_q, slice(t * P, (t + 1) * P), e_q)
            pre.append(acc)

        fetched = []
        for t in range(PACK):
            if t == 0:
                g = late.tile([P, U], F32, name="fetched0", align_bytes=64, offset=starts[2])
            else:
                g = sb([P, U], F32, "x_codes" if t == PACK - 1 else "fetched%d" % t)
            nc.vector.tensor_copy(out=g[:], in_=h[t][:].indirect(whose_sb[:]))
            fetched.append(g)

        w3_staged = late.tile([P, N // P, P, PACK], BF16, name="w3_staged", align_bytes=64, offset=starts[3])
        nc.scalar.copy(
            out=w3_staged[:].rearrange("p h m j -> p m j h"),
            in_=w3_raw[:].rearrange("p j (m h) -> p m j h", h=N // P),
        )
        w3_q = quantize(w3_staged[:].rearrange("p h m j -> p (h m j)"), N, "w3")

        quad = sb([P, 4], F32, "quad")
        nc.gpsimd.tensor_tensor(out=quad[:], in0=risk_group[:, 0, :4], in1=risk_group[:, 1, :4], op=ALU.add)
        pair = sb([P, 2], F32, "pair")
        nc.gpsimd.tensor_tensor(out=pair[:], in0=quad[:, :2], in1=quad[:, 2:], op=ALU.add)
        total = sb([P, 1], F32, "total")
        nc.gpsimd.tensor_tensor(out=total[:], in0=pair[:, :1], in1=pair[:, 1:], op=ALU.add)

        result = sb([P, N // P, U // D], F32, "result")
        turned = [bank(1 + 2 * mh, [P, P]) for mh in range(N // P)]
        for c in range(HALVES):
            planar = sb([P, PACK, HALF], BF16, "planar%d" % c)
            for t in range(PACK):
                nc.vector.scalar_tensor_tensor(
                    out=planar[:, t, :].rearrange("p (v d) -> p v d", d=D // HALVES),
                    in0=pre[t][:].rearrange("p (v c d) -> p c v d", c=HALVES, d=D // HALVES)[:, c],
                    scalar=bias_sb[:, t : t + 1],
                    in1=fetched[t][:].rearrange("p (v c d) -> p c v d", c=HALVES, d=D // HALVES)[:, c],
                    op0=ALU.add,
                    op1=ALU.mult,
                )
            if c == 0:
                inverse = late.tile([P, 1], F32, name="inverse", align_bytes=64, offset=starts[3])
                nc.vector.reciprocal(out=inverse[:], in_=total[:])
                weight = sb([P, HALVES * TILES], F32, "weight")
                nc.gpsimd.tensor_scalar(
                    out=weight[:], in0=risk_group[:, 0, :4], scalar1=inverse[:], scalar2=0.0, op0=ALU.mult, op1=ALU.add
                )
            z = sb([P, TILES, P, PACK], BF16, "z%d" % c)
            src = planar[:].rearrange("p t (m j) -> p m t j", j=TILES)
            dst = z[:].rearrange("p j m t -> p m t j")
            if c == 0:
                nc.scalar.activation(out=dst, in_=src, func=ACT.Relu)
            else:
                nc.vector.tensor_scalar(out=dst[:, :88], in0=src[:, :88], scalar1=0.0, scalar2=None, op0=ALU.max)
                nc.scalar.activation(out=dst[:, 88:], in_=src[:, 88:], func=ACT.Relu)
            z_q = quantize(z[:].rearrange("p j m t -> p (j m t)"), HALF, "z%d" % c)
            weighted = []
            accs = []
            for j in range(TILES):
                acc = bank(2 * j if c == 0 else PACK + j, [P, N])[:]
                product(acc, z_q, slice(j * P, (j + 1) * P), w3_q)
                accs.append(acc)
            for j, acc in enumerate(accs):
                scaled = sb([P, N], F32, "scaled%d_%d" % (c, j))
                if j == 1:
                    nc.vector.tensor_scalar(out=scaled[:], in0=acc, scalar1=weight[:, TILES * c + j : TILES * c + j + 1], scalar2=None, op0=ALU.mult)
                else:
                    nc.scalar.activation(out=scaled[:], in_=acc, func=ACT.Copy, scale=weight[:, TILES * c + j : TILES * c + j + 1])
                weighted.append(scaled)
            for j in range(TILES):
                for mh in range(N // P):
                    nc.tensor.matmul(
                        turned[mh][:],
                        lhsT=weighted[j][:, mh * P : (mh + 1) * P],
                        rhs=identity[:],
                        is_transpose=True,
                        start=(c == 0 and j == 0),
                        stop=(c == HALVES - 1 and j == TILES - 1),
                    )
        for mh in range(N // P):
            nc.vector.tensor_reduce(
                out=result[:, mh, :],
                in_=turned[mh][:].rearrange("p (v s) -> p v s", s=2),
                axis=AXIS.X,
                op=ALU.add,
            )
        nc.sync.dma_start(out=out.rearrange("(p h) v -> p h v", p=P), in_=result[:])
